import numpy as np
import ml_dtypes


def mxq(x, axis, fmt="e4m3"):
    dtype, down = {"e4m3": (ml_dtypes.float8_e4m3fn, 7), "e5m2": (ml_dtypes.float8_e5m2, 14)}[fmt]
    v = np.moveaxis(np.asarray(x, np.float32).astype(ml_dtypes.bfloat16).astype(np.float64), axis, -1)
    blocks = v.reshape(v.shape[:-1] + (-1, 32))
    amax = np.abs(blocks).max(-1, keepdims=True)
    byte = np.maximum(np.where(amax > 0, np.frexp(amax)[1] - 1 + 127, 0) - down, 1)
    scale = np.exp2(byte - 127.0)
    codes = (blocks / scale).astype(np.float32).astype(dtype).astype(np.float64)
    return np.moveaxis((codes * scale).reshape(v.shape), -1, axis)


WIDE = False


def mx_kscale(k):
    if not WIDE:
        return np.ones(k)
    levels = np.array([10, -10, 5, -5, 0])
    if k % 512:
        return np.exp2(np.random.permutation(np.resize(levels, k // 32))).repeat(32)
    a = np.empty((k // 512, 16))
    for p in range(k // 512):
        a[p, :8] = np.random.permutation(np.resize(levels, 8))
        for g in range(8):
            far = levels[np.abs(levels - a[p, g]) >= 10]
            a[p, g + 8] = far[np.random.randint(len(far))]
    return np.exp2(a.ravel()).repeat(32)


def f64(x):
    return np.asarray(x).astype(np.float64)


def striped(idx):
    return np.tile(idx.reshape(-1, 16).T, (8, 1)).astype(np.uint16)


def unstriped(offs):
    return offs[:16].T.reshape(-1).astype(np.int64)


E2M1 = np.array([0.0, 0.5, 1.0, 1.5, 2.0, 3.0, 4.0, 6.0, -0.0, -0.5, -1.0, -1.5, -2.0, -3.0, -4.0, -6.0])


def pack_weight(w, fmt):
    k, n = w.shape
    w = f64(np.asarray(w, np.float32).astype(ml_dtypes.bfloat16)).reshape(k // 32, 32, n)
    amax = np.abs(w).max(1)
    if fmt == "e4m3":
        byte = np.frexp(amax)[1] - 1 + 127 - 7
    else:
        mant, ex = np.frexp(amax / 6.0)
        byte = np.where(mant > 0.5, ex, ex - 1) + 127
    byte = np.clip(np.where(amax > 0, byte, 1), 1, 254)
    scaled = (w * np.exp2(127.0 - byte)[:, None, :]).reshape(k, n).astype(np.float32)
    by_word = np.ascontiguousarray(scaled.reshape(k // 512, 128, 4, n).transpose(0, 1, 3, 2))
    if fmt == "e4m3":
        words = by_word.astype(ml_dtypes.float8_e4m3fn).view(np.uint8)
    else:
        c = by_word.astype(ml_dtypes.float4_e2m1fn).view(np.uint8) & 0xF
        words = (c[..., 0::2] | (c[..., 1::2] << 4)).reshape(k // 512, 128, 2 * n)
    return np.ascontiguousarray(words), np.ascontiguousarray(byte.astype(np.uint8).reshape(k // 512, 16, n))


def unpack_weight(words, scales, fmt):
    g, _, n = scales.shape
    words = np.ascontiguousarray(words).reshape(g, 128, n, -1)
    if fmt == "e4m3":
        vals = words.view(ml_dtypes.float8_e4m3fn).astype(np.float64)
    else:
        nib = np.empty((g, 128, n, 4), np.uint8)
        nib[..., 0::2] = words & 0xF
        nib[..., 1::2] = words >> 4
        vals = E2M1[nib]
    vals = vals * np.repeat(np.exp2(scales.astype(np.float64) - 127.0), 8, axis=1)[..., None]
    return vals.transpose(0, 1, 3, 2).reshape(g * 512, n)


def silu(v):
    return v / (1.0 + np.exp(-np.maximum(v, -700.0)))


K, T, E, C, H, N = 512, 1280, 4, 256, 512, 512


def by_expert(wq, xq):
    return np.concatenate([wq[e].T @ xq[:, e * C:(e + 1) * C] for e in range(E)], axis=1)


def setup_inputs():
    n = np.random.standard_normal
    s = mx_kscale(K)[:, None]
    u = mx_kscale(H)
    w1 = [pack_weight(m, "e2m1") for m in n((E, K, H)) / np.sqrt(K) / s[None]]
    w3 = [pack_weight(m, "e2m1") for m in n((E, K, H)) / np.sqrt(K) / s[None] * u[None, None, :]]
    w2 = [pack_weight(m, "e2m1") for m in n((E, H, N)) / np.sqrt(H) / u[None, :, None]]
    return {
        "xT": (n((K, T)) * s).astype(np.float32),
        "w1_words": np.stack([m[0] for m in w1]),
        "w1_scales": np.stack([m[1] for m in w1]),
        "w3_words": np.stack([m[0] for m in w3]),
        "w3_scales": np.stack([m[1] for m in w3]),
        "w2_words": np.stack([m[0] for m in w2]),
        "w2_scales": np.stack([m[1] for m in w2]),
        "gate": np.tile(np.random.uniform(0.2, 1.0, E * C), (N, 1)).astype(np.float32),
        "offs": striped(np.random.permutation(T)[:E * C]),
        "dst": striped(np.random.permutation(T)[:E * C]),
    }


def reference(xT, w1_words, w1_scales, w3_words, w3_scales, w2_words, w2_scales, gate, offs, dst):
    idx = unstriped(offs)
    w1 = np.stack([unpack_weight(w1_words[e], w1_scales[e], "e2m1") for e in range(E)])
    w3 = np.stack([unpack_weight(w3_words[e], w3_scales[e], "e2m1") for e in range(E)])
    w2 = np.stack([unpack_weight(w2_words[e], w2_scales[e], "e2m1") for e in range(E)])
    xq = mxq(f64(xT)[:, idx], 0, "e4m3")
    h = silu(by_expert(w1, xq))
    h = h * by_expert(w3, xq)
    y = by_expert(w2, mxq(h, 0, "e4m3"))
    out = np.zeros((N, T))
    out[:, unstriped(dst)] = f64(gate) * y
    return out

@@ -1,0 +1,204 @@
+from contextlib import ExitStack
+
+import concourse.mybir as mybir
+from concourse.masks import make_identity
+
+K, T, E, C, H, N = 512, 1280, 4, 256, 512, 512
+P = 128
+PACK = 4
+S = E * C
+N_TILES = N // P
+FLOPS = 2 * S * (K * H + K * H + H * N)
+BYTES = 4 * K * T + 3 * E * (P * 1024 + 16 * 512) + 4 * S + 2 * 2 * S + 4 * N * T
+
+F32 = mybir.dt.float32
+BF16 = mybir.dt.bfloat16
+I32 = mybir.dt.int32
+U32 = mybir.dt.uint32
+U16 = mybir.dt.uint16
+U8 = mybir.dt.uint8
+FP8X4 = mybir.dt.float8_e4m3fn_x4
+FP4X4 = mybir.dt.float4_e2m1fn_x4
+ACT = mybir.ActivationFunctionType
+MULT = mybir.AluOpType.mult
+
+CHUNKS = ((0, 512), (512, 512), (1024, 128), (1152, 128))
+VSHARE = {512: 208, 128: 64}
+
+
+def tile_moe_two_glu_silu_kernel(
+    tc, xT, w1_words, w1_scales, w3_words, w3_scales, w2_words, w2_scales, gate, offs, dst, out
+):
+    nc = tc.nc
+    with ExitStack() as ctx:
+        keep = ctx.enter_context(tc.tile_pool(name="keep", bufs=1))
+        work = ctx.enter_context(tc.tile_pool(name="work", bufs=3))
+        psum = ctx.enter_context(tc.psum_pool(name="psum", bufs=2))
+
+        offs_t = keep.tile([P, S // 16], U16, name="offs_t")
+        dst_t = keep.tile([P, S // 16], U16, name="dst_t")
+
+        x_rows = xT.rearrange("(p j) t -> p j t", j=PACK)
+        raws = []
+        for c, (t0, width) in enumerate(CHUNKS):
+            raw = keep.tile([P, PACK, width], F32, name=f"raw{c}")
+            nc.sync.dma_start(out=raw[:], in_=x_rows[:, :, t0 : t0 + width])
+            raws.append(raw)
+            if c == 1:
+                nc.sync.dma_start(offs_t[:], offs)
+
+        warm = keep.tile([P, 1], F32, name="warm")
+        nc.vector.memset(warm[:], 0.0)
+        warm_out = keep.tile([P, 1], F32, name="warm_out")
+        nc.scalar.activation(warm_out[:], warm[:], ACT.Silu)
+
+        planes = {}
+        for key, scales in (("w1", w1_scales), ("w3", w3_scales), ("w2", w2_scales)):
+            plane = keep.tile([P, E, 512], U8, name=f"plane_{key}", align_bytes=64)
+            nc.vector.memset(plane[:].bitcast(I32), 0)
+            for q in range(4):
+                nc.scalar.dma_start(
+                    out=plane[32 * q : 32 * q + 4, :, :].bitcast(I32),
+                    in_=scales[:, 0, 4 * q : 4 * q + 4, :].rearrange("e q i -> q e i").bitcast(I32),
+                )
+            planes[key] = plane
+
+        words = {}
+
+        def load_words(key, src, e0, e1):
+            t = keep.tile([P, e1 - e0, 1024], U8, name=f"words_{key}_{e0}", align_bytes=64)
+            nc.sync.dma_start(
+                out=t[:].bitcast(I32), in_=src[e0:e1, 0].rearrange("e p b -> p e b").bitcast(I32)
+            )
+            for e in range(e0, e1):
+                words[key, e] = t[:, e - e0, :]
+
+        load_words("w1", w1_words, 0, 1)
+        load_words("w3", w3_words, 0, 1)
+        load_words("w1", w1_words, 1, 4)
+        load_words("w3", w3_words, 1, 4)
+        load_words("w2", w2_words, 0, 4)
+        nc.sync.dma_start(dst_t[:], dst)
+        gate_t = keep.tile([P, S], F32, name="gate_t")
+        nc.sync.dma_start(out=gate_t[:], in_=gate[0:P, :])
+
+        x_words = keep.tile([P, T], U32, name="x_words", align_bytes=64)
+        x_scales = keep.tile([P, T], U8, name="x_scales", align_bytes=64)
+        nc.gpsimd.memset(x_scales[:], 0)
+        ident = keep.tile([P, P], F32, name="ident")
+        make_identity(nc, ident[:])
+
+        windows = []
+        for nt in range(N_TILES):
+            window = keep.tile([P, T], F32, name=f"window{nt}")
+            nc.gpsimd.memset(window[:], 0.0)
+            windows.append(window)
+
+        for c, (t0, width) in enumerate(CHUNKS):
+            grouped = keep.tile([P, width, PACK], BF16, name=f"grouped{c}", align_bytes=64)
+            v = VSHARE[width]
+            for engine_copy, a, b in ((nc.vector.tensor_copy, 0, v), (nc.scalar.copy, v, width)):
+                engine_copy(
+                    out=grouped[:, a:b, :].rearrange("p (c i) t -> p c t i", i=4),
+                    in_=raws[c][:, :, a:b].rearrange("p t (c i) -> p c t i", i=4),
+                )
+            nc.vector.quantize_mx(
+                out=x_words[:, t0 : t0 + width].bitcast(FP8X4),
+                scales=x_scales[:, t0 : t0 + width],
+                in_=grouped[:].rearrange("p w j -> p (w j)"),
+            )
+
+        s_words = keep.tile([P, S], U32, name="s_words", align_bytes=64)
+        s_scales = keep.tile([P, S], U8, name="s_scales", align_bytes=64)
+
+        def gather(e, n=1):
+            sl = slice(e * C, (e + n) * C)
+            ix = offs_t[:, e * (C // 16) : (e + n) * (C // 16)]
+            nc.vector.tensor_copy(s_words[:, sl], x_words[:].indirect(ix))
+            nc.vector.tensor_copy(s_scales[:, sl], x_scales[:].indirect(ix))
+
+        def first(e):
+            ht_ps = psum.tile([P, 2, C], F32, name="ht_ps", bufs=1)
+            for g in range(C // P):
+                s0 = e * C + g * P
+                a_ps = psum.tile([P, H], F32, name="a_ps")
+                b_ps = psum.tile([P, H], F32, name="b_ps")
+                for acc, key in ((a_ps, "w1"), (b_ps, "w3")):
+                    nc.tensor.matmul_mx(
+                        out=acc[:],
+                        lhsT=s_words[:, s0 : s0 + P].bitcast(FP8X4),
+                        lhsT_scale=s_scales[:, s0 : s0 + P],
+                        rhs=words[key, e].bitcast(FP4X4),
+                        rhs_scale=planes[key][:, e, :],
+                        start=True,
+                        stop=True,
+                    )
+                act = work.tile([P, H], F32, name="act")
+                nc.scalar.activation(
+                    act[:].rearrange("s (u p e) -> s u p e", u=2, e=2),
+                    a_ps[:].rearrange("s (p u e) -> s u p e", u=2, e=2),
+                    ACT.Silu,
+                )
+                h = work.tile([P, H], BF16, name="h", align_bytes=64)
+                nc.vector.tensor_tensor(
+                    h[:].rearrange("s (u p e) -> s u p e", u=2, e=2),
+                    b_ps[:].rearrange("s (p u e) -> s u p e", u=2, e=2),
+                    act[:].rearrange("s (u p e) -> s u p e", u=2, e=2),
+                    MULT,
+                )
+                for u in range(2):
+                    nc.tensor.transpose(
+                        ht_ps[:, u, g * P : (g + 1) * P], h[:, u * 256 : (u + 1) * 256].bitcast(F32), ident[:]
+                    )
+            hg = work.tile([P, C * PACK], BF16, name="hg", align_bytes=64)
+            nc.scalar.copy(
+                out=hg[:].bitcast(F32).rearrange("p (r u) -> p r u", u=2),
+                in_=ht_ps[:].rearrange("p u r -> p r u"),
+            )
+            h_words = work.tile([P, C], U32, name="h_words", align_bytes=64)
+            h_scales = work.tile([P, C], U8, name="h_scales", align_bytes=64)
+            nc.vector.quantize_mx(out=h_words[:].bitcast(FP8X4), scales=h_scales[:], in_=hg[:])
+            return h_words, h_scales
+
+        def second(e, h_words, h_scales, y):
+            for half in range(2):
+                y_ps = psum.tile([P, 2, C], F32, name="y_ps", bufs=3)
+                for k in range(2):
+                    nt = 2 * half + k
+                    nc.tensor.matmul_mx(
+                        out=y_ps[:, k, :],
+                        lhsT=words["w2", e][:, nt * 256 : (nt + 1) * 256].bitcast(FP4X4),
+                        lhsT_scale=planes["w2"][:, e, nt * P : (nt + 1) * P],
+                        rhs=h_words[:].bitcast(FP8X4),
+                        rhs_scale=h_scales[:],
+                        start=True,
+                        stop=True,
+                    )
+                nc.scalar.copy(out=y[:, 2 * half : 2 * half + 2, :], in_=y_ps[:])
+
+        def scatter(e, n, y):
+            ix = dst_t[:, e * (C // 16) : (e + n) * (C // 16)]
+            for nt in range(N_TILES):
+                nc.vector.tensor_tensor(
+                    windows[nt][:].indirect(ix), y[:, nt, :], gate_t[:, e * C : (e + n) * C], MULT
+                )
+                if e + n == E:
+                    nc.sync.dma_start(out=out[nt * P : (nt + 1) * P, :], in_=windows[nt][:])
+
+        y0 = keep.tile([P, N_TILES, C], F32, name="y0")
+        y1 = keep.tile([P, N_TILES, C], F32, name="y1")
+        y23 = keep.tile([P, N_TILES, 2 * C], F32, name="y23")
+        gather(0)
+        hw = first(0)
+        gather(1)
+        second(0, *hw, y0[:])
+        gather(2, 2)
+        hw = first(1)
+        second(1, *hw, y1[:])
+        scatter(0, 1, y0)
+        hw = first(2)
+        second(2, *hw, y23[:, :, 0:C])
+        hw = first(3)
+        second(3, *hw, y23[:, :, C : 2 * C])
+        scatter(1, 1, y1)
+        scatter(2, 2, y23)

@@ -22,8 +22,8 @@ FP4X4 = mybir.dt.float4_e2m1fn_x4
 ACT = mybir.ActivationFunctionType
 MULT = mybir.AluOpType.mult
 
-CHUNKS = ((0, 512), (512, 512), (1024, 128), (1152, 128))
-VSHARE = {512: 208, 128: 64}
+CHUNKS = ((0, 512), (512, 512), (1024, 256))
+VSHARE = {512: 208, 256: 112}
 
 
 def tile_moe_two_glu_silu_kernel(
@@ -33,10 +33,24 @@ def tile_moe_two_glu_silu_kernel(
     with ExitStack() as ctx:
         keep = ctx.enter_context(tc.tile_pool(name="keep", bufs=1))
         work = ctx.enter_context(tc.tile_pool(name="work", bufs=3))
+        hold = ctx.enter_context(tc.tile_pool(name="hold", bufs=1))
         psum = ctx.enter_context(tc.psum_pool(name="psum", bufs=2))
 
         offs_t = keep.tile([P, S // 16], U16, name="offs_t")
         dst_t = keep.tile([P, S // 16], U16, name="dst_t")
+
+        planes = {}
+        for key in ("w1", "w3", "w2"):
+            plane = keep.tile([P, E, 512], U8, name=f"plane_{key}", align_bytes=64)
+            nc.vector.memset(plane[:].bitcast(I32), 0)
+            planes[key] = plane
+
+        def load_scales(queue, key, scales):
+            for q in range(4):
+                queue.dma_start(
+                    out=planes[key][32 * q : 32 * q + 4, :, :].bitcast(I32),
+                    in_=scales[:, 0, 4 * q : 4 * q + 4, :].rearrange("e q i -> q e i").bitcast(I32),
+                )
 
         x_rows = xT.rearrange("(p j) t -> p j t", j=PACK)
         raws = []
@@ -44,24 +58,14 @@ def tile_moe_two_glu_silu_kernel(
             raw = keep.tile([P, PACK, width], F32, name=f"raw{c}")
             nc.sync.dma_start(out=raw[:], in_=x_rows[:, :, t0 : t0 + width])
             raws.append(raw)
-            if c == 1:
-                nc.sync.dma_start(offs_t[:], offs)
+        nc.sync.dma_start(offs_t[:], offs)
+        load_scales(nc.sync, "w1", w1_scales)
+        load_scales(nc.gpsimd, "w3", w3_scales)
 
         warm = keep.tile([P, 1], F32, name="warm")
         nc.vector.memset(warm[:], 0.0)
         warm_out = keep.tile([P, 1], F32, name="warm_out")
         nc.scalar.activation(warm_out[:], warm[:], ACT.Silu)
-
-        planes = {}
-        for key, scales in (("w1", w1_scales), ("w3", w3_scales), ("w2", w2_scales)):
-            plane = keep.tile([P, E, 512], U8, name=f"plane_{key}", align_bytes=64)
-            nc.vector.memset(plane[:].bitcast(I32), 0)
-            for q in range(4):
-                nc.scalar.dma_start(
-                    out=plane[32 * q : 32 * q + 4, :, :].bitcast(I32),
-                    in_=scales[:, 0, 4 * q : 4 * q + 4, :].rearrange("e q i -> q e i").bitcast(I32),
-                )
-            planes[key] = plane
 
         words = {}
 
@@ -77,6 +81,7 @@ def tile_moe_two_glu_silu_kernel(
         load_words("w3", w3_words, 0, 1)
         load_words("w1", w1_words, 1, 4)
         load_words("w3", w3_words, 1, 4)
+        load_scales(nc.sync, "w2", w2_scales)
         load_words("w2", w2_words, 0, 4)
         nc.sync.dma_start(dst_t[:], dst)
         gate_t = keep.tile([P, S], F32, name="gate_t")
@@ -91,7 +96,7 @@ def tile_moe_two_glu_silu_kernel(
         windows = []
         for nt in range(N_TILES):
             window = keep.tile([P, T], F32, name=f"window{nt}")
-            nc.gpsimd.memset(window[:], 0.0)
+            (nc.vector if nt < 2 else nc.gpsimd).memset(window[:], 0.0)
             windows.append(window)
 
         for c, (t0, width) in enumerate(CHUNKS):
@@ -140,23 +145,31 @@ def tile_moe_two_glu_silu_kernel(
                     ACT.Silu,
                 )
                 h = work.tile([P, H], BF16, name="h", align_bytes=64)
-                nc.vector.tensor_tensor(
-                    h[:].rearrange("s (u p e) -> s u p e", u=2, e=2),
-                    b_ps[:].rearrange("s (p u e) -> s u p e", u=2, e=2),
-                    act[:].rearrange("s (u p e) -> s u p e", u=2, e=2),
-                    MULT,
-                )
+                if e == 0:
+                    nc.vector.tensor_tensor(
+                        h[:].rearrange("s (u p e) -> s u p e", u=2, e=2),
+                        b_ps[:].rearrange("s (p u e) -> s u p e", u=2, e=2),
+                        act[:].rearrange("s (u p e) -> s u p e", u=2, e=2),
+                        MULT,
+                    )
+                else:
+                    lin = work.tile([P, H], F32, name="lin")
+                    nc.scalar.copy(
+                        out=lin[:].rearrange("s (u p e) -> s u p e", u=2, e=2),
+                        in_=b_ps[:].rearrange("s (p u e) -> s u p e", u=2, e=2),
+                    )
+                    nc.gpsimd.tensor_tensor(h[:], lin[:], act[:], MULT)
                 for u in range(2):
                     nc.tensor.transpose(
                         ht_ps[:, u, g * P : (g + 1) * P], h[:, u * 256 : (u + 1) * 256].bitcast(F32), ident[:]
                     )
-            hg = work.tile([P, C * PACK], BF16, name="hg", align_bytes=64)
+            hg = hold.tile([P, C * PACK], BF16, name=f"hg{e}", tag=f"hold{e}", align_bytes=64)
             nc.scalar.copy(
                 out=hg[:].bitcast(F32).rearrange("p (r u) -> p r u", u=2),
                 in_=ht_ps[:].rearrange("p u r -> p r u"),
             )
-            h_words = work.tile([P, C], U32, name="h_words", align_bytes=64)
-            h_scales = work.tile([P, C], U8, name="h_scales", align_bytes=64)
+            h_words = keep.tile([P, C], U32, name=f"h_words{e}", align_bytes=64)
+            h_scales = keep.tile([P, C], U8, name=f"h_scales{e}", align_bytes=64)
             nc.vector.quantize_mx(out=h_words[:].bitcast(FP8X4), scales=h_scales[:], in_=hg[:])
             return h_words, h_scales
 
@@ -174,31 +187,46 @@ def tile_moe_two_glu_silu_kernel(
                         start=True,
                         stop=True,
                     )
-                nc.scalar.copy(out=y[:, 2 * half : 2 * half + 2, :], in_=y_ps[:])
+                gates = gate_t[:, e * C : (e + 1) * C]
+                if e == 0:
+                    for k in range(2):
+                        nc.vector.tensor_tensor(y[2 * half + k], y_ps[:, k, :], gates, MULT)
+                else:
+                    raw_y = work.tile([P, 2, C], F32, name="raw_y")
+                    nc.scalar.copy(out=raw_y[:], in_=y_ps[:])
+                    for k in range(2):
+                        nc.gpsimd.tensor_tensor(y[2 * half + k], raw_y[:, k, :], gates, MULT)
 
         def scatter(e, n, y):
             ix = dst_t[:, e * (C // 16) : (e + n) * (C // 16)]
             for nt in range(N_TILES):
-                nc.vector.tensor_tensor(
-                    windows[nt][:].indirect(ix), y[:, nt, :], gate_t[:, e * C : (e + n) * C], MULT
-                )
+                nc.vector.tensor_copy(windows[nt][:].indirect(ix), y[nt])
                 if e + n == E:
                     nc.sync.dma_start(out=out[nt * P : (nt + 1) * P, :], in_=windows[nt][:])
 
-        y0 = keep.tile([P, N_TILES, C], F32, name="y0")
-        y1 = keep.tile([P, N_TILES, C], F32, name="y1")
-        y23 = keep.tile([P, N_TILES, 2 * C], F32, name="y23")
+        def results(e, width, after):
+            tiles = []
+            for nt in range(N_TILES):
+                y = hold.tile([P, width], F32, name=f"y{e}_{nt}", tag=after.get(nt, f"y{e}_{nt}"), align_bytes=64)
+                tiles.append(y)
+            return tiles
+
         gather(0)
-        hw = first(0)
+        hw0 = first(0)
         gather(1)
-        second(0, *hw, y0[:])
+        hw1 = first(1)
         gather(2, 2)
-        hw = first(1)
-        second(1, *hw, y1[:])
-        scatter(0, 1, y0)
-        hw = first(2)
-        second(2, *hw, y23[:, :, 0:C])
-        hw = first(3)
-        second(3, *hw, y23[:, :, C : 2 * C])
-        scatter(1, 1, y1)
-        scatter(2, 2, y23)
+        hw2 = first(2)
+        y0 = results(0, C, {2: "hold1", 3: "hold2"})
+        second(0, *hw0, [y[:] for y in y0])
+        scatter(0, 1, [y[:] for y in y0])
+        hw3 = first(3)
+        y1 = results(1, C, {3: "hold3"})
+        second(1, *hw1, [y[:] for y in y1])
+        scatter(1, 1, [y[:] for y in y1])
+        y2 = results(2, C, {})
+        second(2, *hw2, [y[:] for y in y2])
+        scatter(2, 1, [y[:] for y in y2])
+        y3 = results(3, C, {})
+        second(3, *hw3, [y[:] for y in y3])
+        scatter(3, 1, [y[:] for y in y3])

@@ -23,7 +23,7 @@ ACT = mybir.ActivationFunctionType
 MULT = mybir.AluOpType.mult
 
 CHUNKS = ((0, 512), (512, 512), (1024, 256))
-VSHARE = {512: 208, 256: 112}
+VSHARE = {512: 344, 256: 168}
 
 
 def tile_moe_two_glu_silu_kernel(
@@ -44,6 +44,8 @@ def tile_moe_two_glu_silu_kernel(
             plane = keep.tile([P, E, 512], U8, name=f"plane_{key}", align_bytes=64)
             nc.vector.memset(plane[:].bitcast(I32), 0)
             planes[key] = plane
+        x_scales = keep.tile([P, T], U8, name="x_scales", align_bytes=64)
+        nc.vector.memset(x_scales[:].bitcast(I32), 0)
 
         def load_scales(queue, key, scales):
             for q in range(4):
@@ -51,21 +53,6 @@ def tile_moe_two_glu_silu_kernel(
                     out=planes[key][32 * q : 32 * q + 4, :, :].bitcast(I32),
                     in_=scales[:, 0, 4 * q : 4 * q + 4, :].rearrange("e q i -> q e i").bitcast(I32),
                 )
-
-        x_rows = xT.rearrange("(p j) t -> p j t", j=PACK)
-        raws = []
-        for c, (t0, width) in enumerate(CHUNKS):
-            raw = keep.tile([P, PACK, width], F32, name=f"raw{c}")
-            nc.sync.dma_start(out=raw[:], in_=x_rows[:, :, t0 : t0 + width])
-            raws.append(raw)
-        nc.sync.dma_start(offs_t[:], offs)
-        load_scales(nc.sync, "w1", w1_scales)
-        load_scales(nc.gpsimd, "w3", w3_scales)
-
-        warm = keep.tile([P, 1], F32, name="warm")
-        nc.vector.memset(warm[:], 0.0)
-        warm_out = keep.tile([P, 1], F32, name="warm_out")
-        nc.scalar.activation(warm_out[:], warm[:], ACT.Silu)
 
         words = {}
 
@@ -77,27 +64,42 @@ def tile_moe_two_glu_silu_kernel(
             for e in range(e0, e1):
                 words[key, e] = t[:, e - e0, :]
 
+        x_rows = xT.rearrange("(p j) t -> p j t", j=PACK)
+        raws = []
+        for c, (t0, width) in enumerate(CHUNKS):
+            raw = keep.tile([P, PACK, width], F32, name=f"raw{c}", align_bytes=64)
+            nc.sync.dma_start(out=raw[:], in_=x_rows[:, :, t0 : t0 + width])
+            raws.append(raw)
+        nc.sync.dma_start(offs_t[:], offs)
+        load_scales(nc.gpsimd, "w1", w1_scales)
+        load_scales(nc.gpsimd, "w3", w3_scales)
         load_words("w1", w1_words, 0, 1)
         load_words("w3", w3_words, 0, 1)
+        load_scales(nc.sync, "w2", w2_scales)
         load_words("w1", w1_words, 1, 4)
         load_words("w3", w3_words, 1, 4)
-        load_scales(nc.sync, "w2", w2_scales)
         load_words("w2", w2_words, 0, 4)
         nc.sync.dma_start(dst_t[:], dst)
         gate_t = keep.tile([P, S], F32, name="gate_t")
         nc.sync.dma_start(out=gate_t[:], in_=gate[0:P, :])
 
-        x_words = keep.tile([P, T], U32, name="x_words", align_bytes=64)
-        x_scales = keep.tile([P, T], U8, name="x_scales", align_bytes=64)
-        nc.gpsimd.memset(x_scales[:], 0)
-        ident = keep.tile([P, P], F32, name="ident")
-        make_identity(nc, ident[:])
+        warm = keep.tile([P, 1], F32, name="warm")
+        nc.vector.memset(warm[:], 0.0)
+        warm_out = keep.tile([P, 1], F32, name="warm_out")
+        nc.scalar.activation(warm_out[:], warm[:], ACT.Silu)
 
         windows = []
         for nt in range(N_TILES):
-            window = keep.tile([P, T], F32, name=f"window{nt}")
-            (nc.vector if nt < 2 else nc.gpsimd).memset(window[:], 0.0)
+            window = keep.tile([P, T], F32, name=f"window{nt}", align_bytes=64)
+            if nt < 2:
+                nc.vector.memset(window[:], 0.0)
+            else:
+                nc.scalar.copy(out=window[:], in_=warm[:].to_broadcast([P, T]))
             windows.append(window)
+
+        x_words = keep.tile([P, T], U32, name="x_words", align_bytes=64)
+        ident = keep.tile([P, P], F32, name="ident")
+        make_identity(nc, ident[:])
 
         for c, (t0, width) in enumerate(CHUNKS):
             grouped = keep.tile([P, width, PACK], BF16, name=f"grouped{c}", align_bytes=64)

@@ -22,8 +22,8 @@ FP4X4 = mybir.dt.float4_e2m1fn_x4
 ACT = mybir.ActivationFunctionType
 MULT = mybir.AluOpType.mult
 
-CHUNKS = ((0, 512), (512, 512), (1024, 256))
-VSHARE = {512: 344, 256: 168}
+CHUNKS = ((0, 512), (512, 512), (1024, 128), (1152, 128))
+VSHARE = {512: 344, 128: 84}
 
 
 def tile_moe_two_glu_silu_kernel(
@@ -115,32 +115,36 @@ def tile_moe_two_glu_silu_kernel(
                 in_=grouped[:].rearrange("p w j -> p (w j)"),
             )
 
-        s_words = keep.tile([P, S], U32, name="s_words", align_bytes=64)
-        s_scales = keep.tile([P, S], U8, name="s_scales", align_bytes=64)
+        s_words, s_scales = {}, {}
 
-        def gather(e, n=1):
-            sl = slice(e * C, (e + n) * C)
-            ix = offs_t[:, e * (C // 16) : (e + n) * (C // 16)]
-            nc.vector.tensor_copy(s_words[:, sl], x_words[:].indirect(ix))
-            nc.vector.tensor_copy(s_scales[:, sl], x_scales[:].indirect(ix))
+        def gather(e):
+            ix = offs_t[:, e * (C // 16) : (e + 1) * (C // 16)]
+            tag = {2: "act00", 3: "act01"}.get(e, f"s_words{e}")
+            s_w = hold.tile([P, C], U32, name=f"s_words{e}", tag=tag, align_bytes=64)
+            s_s = keep.tile([P, C], U8, name=f"s_scales{e}", align_bytes=64)
+            nc.vector.tensor_copy(s_w[:], x_words[:].indirect(ix))
+            nc.vector.tensor_copy(s_s[:], x_scales[:].indirect(ix))
+            s_words[e], s_scales[e] = s_w, s_s
 
         def first(e):
             ht_ps = psum.tile([P, 2, C], F32, name="ht_ps", bufs=1)
             for g in range(C // P):
-                s0 = e * C + g * P
+                slots = slice(g * P, (g + 1) * P)
                 a_ps = psum.tile([P, H], F32, name="a_ps")
                 b_ps = psum.tile([P, H], F32, name="b_ps")
                 for acc, key in ((a_ps, "w1"), (b_ps, "w3")):
                     nc.tensor.matmul_mx(
                         out=acc[:],
-                        lhsT=s_words[:, s0 : s0 + P].bitcast(FP8X4),
-                        lhsT_scale=s_scales[:, s0 : s0 + P],
+                        lhsT=s_words[e][:, slots].bitcast(FP8X4),
+                        lhsT_scale=s_scales[e][:, slots],
                         rhs=words[key, e].bitcast(FP4X4),
                         rhs_scale=planes[key][:, e, :],
                         start=True,
                         stop=True,
                     )
-                act = work.tile([P, H], F32, name="act")
+                tag = {(0, 0): "act00", (0, 1): "act01", (1, 0): "hold0"}.get((e, g), "act")
+                pool = work if tag == "act" else hold
+                act = pool.tile([P, H], F32, name=f"act{e}{g}", tag=tag, align_bytes=64)
                 nc.scalar.activation(
                     act[:].rearrange("s (u p e) -> s u p e", u=2, e=2),
                     a_ps[:].rearrange("s (p u e) -> s u p e", u=2, e=2),
@@ -166,13 +170,17 @@ def tile_moe_two_glu_silu_kernel(
                         ht_ps[:, u, g * P : (g + 1) * P], h[:, u * 256 : (u + 1) * 256].bitcast(F32), ident[:]
                     )
             hg = hold.tile([P, C * PACK], BF16, name=f"hg{e}", tag=f"hold{e}", align_bytes=64)
-            nc.scalar.copy(
-                out=hg[:].bitcast(F32).rearrange("p (r u) -> p r u", u=2),
-                in_=ht_ps[:].rearrange("p u r -> p r u"),
-            )
             h_words = keep.tile([P, C], U32, name=f"h_words{e}", align_bytes=64)
             h_scales = keep.tile([P, C], U8, name=f"h_scales{e}", align_bytes=64)
-            nc.vector.quantize_mx(out=h_words[:].bitcast(FP8X4), scales=h_scales[:], in_=hg[:])
+            step = P if e == 0 else C
+            for r0 in range(0, C, step):
+                rows = slice(r0, r0 + step)
+                part = hg[:, r0 * PACK : (r0 + step) * PACK]
+                nc.scalar.copy(
+                    out=part.bitcast(F32).rearrange("p (r u) -> p r u", u=2),
+                    in_=ht_ps[:, :, rows].rearrange("p u r -> p r u"),
+                )
+                nc.vector.quantize_mx(out=h_words[:, rows].bitcast(FP8X4), scales=h_scales[:, rows], in_=part)
             return h_words, h_scales
 
         def second(e, h_words, h_scales, y):
@@ -216,19 +224,20 @@ def tile_moe_two_glu_silu_kernel(
         gather(0)
         hw0 = first(0)
         gather(1)
+        gather(2)
+        gather(3)
         hw1 = first(1)
-        gather(2, 2)
         hw2 = first(2)
-        y0 = results(0, C, {2: "hold1", 3: "hold2"})
+        y0 = results(0, C, {3: "hold1"})
         second(0, *hw0, [y[:] for y in y0])
-        scatter(0, 1, [y[:] for y in y0])
-        hw3 = first(3)
-        y1 = results(1, C, {3: "hold3"})
+        y1 = results(1, C, {})
         second(1, *hw1, [y[:] for y in y1])
-        scatter(1, 1, [y[:] for y in y1])
-        y2 = results(2, C, {})
+        hw3 = first(3)
+        scatter(0, 1, [y[:] for y in y0])
+        y2 = results(2, C, {1: "hold3"})
         second(2, *hw2, [y[:] for y in y2])
-        scatter(2, 1, [y[:] for y in y2])
+        scatter(1, 1, [y[:] for y in y1])
         y3 = results(3, C, {})
         second(3, *hw3, [y[:] for y in y3])
+        scatter(2, 1, [y[:] for y in y2])
         scatter(3, 1, [y[:] for y in y3])

from contextlib import ExitStack

import concourse.mybir as mybir
from concourse.masks import make_identity

K, T, E, C, H, N = 512, 1280, 4, 256, 512, 512
P = 128
PACK = 4
S = E * C
N_TILES = N // P
FLOPS = 2 * S * (K * H + K * H + H * N)
BYTES = 4 * K * T + 3 * E * (P * 1024 + 16 * 512) + 4 * S + 2 * 2 * S + 4 * N * T

F32 = mybir.dt.float32
BF16 = mybir.dt.bfloat16
I32 = mybir.dt.int32
U32 = mybir.dt.uint32
U16 = mybir.dt.uint16
U8 = mybir.dt.uint8
FP8X4 = mybir.dt.float8_e4m3fn_x4
FP4X4 = mybir.dt.float4_e2m1fn_x4
ACT = mybir.ActivationFunctionType
MULT = mybir.AluOpType.mult

CHUNKS = ((0, 512), (512, 512), (1024, 128), (1152, 128))
VSHARE = {512: 344, 128: 84}


def tile_moe_two_glu_silu_kernel(
    tc, xT, w1_words, w1_scales, w3_words, w3_scales, w2_words, w2_scales, gate, offs, dst, out
):
    nc = tc.nc
    with ExitStack() as ctx:
        keep = ctx.enter_context(tc.tile_pool(name="keep", bufs=1))
        work = ctx.enter_context(tc.tile_pool(name="work", bufs=3))
        hold = ctx.enter_context(tc.tile_pool(name="hold", bufs=1))
        psum = ctx.enter_context(tc.psum_pool(name="psum", bufs=2))

        offs_t = keep.tile([P, S // 16], U16, name="offs_t")
        dst_t = keep.tile([P, S // 16], U16, name="dst_t")

        planes = {}
        for key in ("w1", "w3", "w2"):
            plane = keep.tile([P, E, 512], U8, name=f"plane_{key}", align_bytes=64)
            nc.vector.memset(plane[:].bitcast(I32), 0)
            planes[key] = plane
        x_scales = keep.tile([P, T], U8, name="x_scales", align_bytes=64)
        nc.vector.memset(x_scales[:].bitcast(I32), 0)

        def load_scales(queue, key, scales):
            for q in range(4):
                queue.dma_start(
                    out=planes[key][32 * q : 32 * q + 4, :, :].bitcast(I32),
                    in_=scales[:, 0, 4 * q : 4 * q + 4, :].rearrange("e q i -> q e i").bitcast(I32),
                )

        words = {}

        def load_words(key, src, e0, e1):
            t = keep.tile([P, e1 - e0, 1024], U8, name=f"words_{key}_{e0}", align_bytes=64)
            nc.sync.dma_start(
                out=t[:].bitcast(I32), in_=src[e0:e1, 0].rearrange("e p b -> p e b").bitcast(I32)
            )
            for e in range(e0, e1):
                words[key, e] = t[:, e - e0, :]

        x_rows = xT.rearrange("(p j) t -> p j t", j=PACK)
        raws = []
        for c, (t0, width) in enumerate(CHUNKS):
            raw = keep.tile([P, PACK, width], F32, name=f"raw{c}", align_bytes=64)
            nc.sync.dma_start(out=raw[:], in_=x_rows[:, :, t0 : t0 + width])
            raws.append(raw)
        nc.sync.dma_start(offs_t[:], offs)
        load_scales(nc.gpsimd, "w1", w1_scales)
        load_scales(nc.gpsimd, "w3", w3_scales)
        load_words("w1", w1_words, 0, 1)
        load_words("w3", w3_words, 0, 1)
        load_scales(nc.sync, "w2", w2_scales)
        load_words("w1", w1_words, 1, 4)
        load_words("w3", w3_words, 1, 4)
        load_words("w2", w2_words, 0, 4)
        nc.sync.dma_start(dst_t[:], dst)
        gate_t = keep.tile([P, S], F32, name="gate_t")
        nc.sync.dma_start(out=gate_t[:], in_=gate[0:P, :])

        warm = keep.tile([P, 1], F32, name="warm")
        nc.vector.memset(warm[:], 0.0)
        warm_out = keep.tile([P, 1], F32, name="warm_out")
        nc.scalar.activation(warm_out[:], warm[:], ACT.Silu)

        windows = []
        for nt in range(N_TILES):
            window = keep.tile([P, T], F32, name=f"window{nt}", align_bytes=64)
            if nt < 2:
                nc.vector.memset(window[:], 0.0)
            else:
                nc.scalar.copy(out=window[:], in_=warm[:].to_broadcast([P, T]))
            windows.append(window)

        x_words = keep.tile([P, T], U32, name="x_words", align_bytes=64)
        ident = keep.tile([P, P], F32, name="ident")
        make_identity(nc, ident[:])

        for c, (t0, width) in enumerate(CHUNKS):
            grouped = keep.tile([P, width, PACK], BF16, name=f"grouped{c}", align_bytes=64)
            v = VSHARE[width]
            for engine_copy, a, b in ((nc.vector.tensor_copy, 0, v), (nc.scalar.copy, v, width)):
                engine_copy(
                    out=grouped[:, a:b, :].rearrange("p (c i) t -> p c t i", i=4),
                    in_=raws[c][:, :, a:b].rearrange("p t (c i) -> p c t i", i=4),
                )
            nc.vector.quantize_mx(
                out=x_words[:, t0 : t0 + width].bitcast(FP8X4),
                scales=x_scales[:, t0 : t0 + width],
                in_=grouped[:].rearrange("p w j -> p (w j)"),
            )

        s_words, s_scales = {}, {}

        def gather(e):
            ix = offs_t[:, e * (C // 16) : (e + 1) * (C // 16)]
            tag = {2: "act00", 3: "act01"}.get(e, f"s_words{e}")
            s_w = hold.tile([P, C], U32, name=f"s_words{e}", tag=tag, align_bytes=64)
            s_s = keep.tile([P, C], U8, name=f"s_scales{e}", align_bytes=64)
            nc.vector.tensor_copy(s_w[:], x_words[:].indirect(ix))
            nc.vector.tensor_copy(s_s[:], x_scales[:].indirect(ix))
            s_words[e], s_scales[e] = s_w, s_s

        def first(e):
            ht_ps = psum.tile([P, 2, C], F32, name="ht_ps", bufs=1)
            for g in range(C // P):
                slots = slice(g * P, (g + 1) * P)
                a_ps = psum.tile([P, H], F32, name="a_ps")
                b_ps = psum.tile([P, H], F32, name="b_ps")
                for acc, key in ((a_ps, "w1"), (b_ps, "w3")):
                    nc.tensor.matmul_mx(
                        out=acc[:],
                        lhsT=s_words[e][:, slots].bitcast(FP8X4),
                        lhsT_scale=s_scales[e][:, slots],
                        rhs=words[key, e].bitcast(FP4X4),
                        rhs_scale=planes[key][:, e, :],
                        start=True,
                        stop=True,
                    )
                tag = {(0, 0): "act00", (0, 1): "act01", (1, 0): "hold0"}.get((e, g), "act")
                pool = work if tag == "act" else hold
                act = pool.tile([P, H], F32, name=f"act{e}{g}", tag=tag, align_bytes=64)
                nc.scalar.activation(
                    act[:].rearrange("s (u p e) -> s u p e", u=2, e=2),
                    a_ps[:].rearrange("s (p u e) -> s u p e", u=2, e=2),
                    ACT.Silu,
                )
                h = work.tile([P, H], BF16, name="h", align_bytes=64)
                if e == 0:
                    nc.vector.tensor_tensor(
                        h[:].rearrange("s (u p e) -> s u p e", u=2, e=2),
                        b_ps[:].rearrange("s (p u e) -> s u p e", u=2, e=2),
                        act[:].rearrange("s (u p e) -> s u p e", u=2, e=2),
                        MULT,
                    )
                else:
                    lin = work.tile([P, H], F32, name="lin")
                    nc.scalar.copy(
                        out=lin[:].rearrange("s (u p e) -> s u p e", u=2, e=2),
                        in_=b_ps[:].rearrange("s (p u e) -> s u p e", u=2, e=2),
                    )
                    nc.gpsimd.tensor_tensor(h[:], lin[:], act[:], MULT)
                for u in range(2):
                    nc.tensor.transpose(
                        ht_ps[:, u, g * P : (g + 1) * P], h[:, u * 256 : (u + 1) * 256].bitcast(F32), ident[:]
                    )
            hg = hold.tile([P, C * PACK], BF16, name=f"hg{e}", tag=f"hold{e}", align_bytes=64)
            h_words = keep.tile([P, C], U32, name=f"h_words{e}", align_bytes=64)
            h_scales = keep.tile([P, C], U8, name=f"h_scales{e}", align_bytes=64)
            step = P if e == 0 else C
            for r0 in range(0, C, step):
                rows = slice(r0, r0 + step)
                part = hg[:, r0 * PACK : (r0 + step) * PACK]
                nc.scalar.copy(
                    out=part.bitcast(F32).rearrange("p (r u) -> p r u", u=2),
                    in_=ht_ps[:, :, rows].rearrange("p u r -> p r u"),
                )
                nc.vector.quantize_mx(out=h_words[:, rows].bitcast(FP8X4), scales=h_scales[:, rows], in_=part)
            return h_words, h_scales

        def second(e, h_words, h_scales, y):
            for half in range(2):
                y_ps = psum.tile([P, 2, C], F32, name="y_ps", bufs=3)
                for k in range(2):
                    nt = 2 * half + k
                    nc.tensor.matmul_mx(
                        out=y_ps[:, k, :],
                        lhsT=words["w2", e][:, nt * 256 : (nt + 1) * 256].bitcast(FP4X4),
                        lhsT_scale=planes["w2"][:, e, nt * P : (nt + 1) * P],
                        rhs=h_words[:].bitcast(FP8X4),
                        rhs_scale=h_scales[:],
                        start=True,
                        stop=True,
                    )
                gates = gate_t[:, e * C : (e + 1) * C]
                if e == 0:
                    for k in range(2):
                        nc.vector.tensor_tensor(y[2 * half + k], y_ps[:, k, :], gates, MULT)
                else:
                    raw_y = work.tile([P, 2, C], F32, name="raw_y")
                    nc.scalar.copy(out=raw_y[:], in_=y_ps[:])
                    for k in range(2):
                        nc.gpsimd.tensor_tensor(y[2 * half + k], raw_y[:, k, :], gates, MULT)

        def scatter(e, n, y):
            ix = dst_t[:, e * (C // 16) : (e + n) * (C // 16)]
            for nt in range(N_TILES):
                nc.vector.tensor_copy(windows[nt][:].indirect(ix), y[nt])
                if e + n == E:
                    nc.sync.dma_start(out=out[nt * P : (nt + 1) * P, :], in_=windows[nt][:])

        def results(e, width, after):
            tiles = []
            for nt in range(N_TILES):
                y = hold.tile([P, width], F32, name=f"y{e}_{nt}", tag=after.get(nt, f"y{e}_{nt}"), align_bytes=64)
                tiles.append(y)
            return tiles

        gather(0)
        hw0 = first(0)
        gather(1)
        gather(2)
        gather(3)
        hw1 = first(1)
        hw2 = first(2)
        y0 = results(0, C, {3: "hold1"})
        second(0, *hw0, [y[:] for y in y0])
        y1 = results(1, C, {})
        second(1, *hw1, [y[:] for y in y1])
        hw3 = first(3)
        scatter(0, 1, [y[:] for y in y0])
        y2 = results(2, C, {1: "hold3"})
        second(2, *hw2, [y[:] for y in y2])
        scatter(1, 1, [y[:] for y in y1])
        y3 = results(3, C, {})
        second(3, *hw3, [y[:] for y in y3])
        scatter(2, 1, [y[:] for y in y2])
        scatter(3, 1, [y[:] for y in y3])
